import numpy as np
import ml_dtypes


def mxq(x, axis, fmt="e4m3"):
    dtype, down = {"e4m3": (ml_dtypes.float8_e4m3fn, 7), "e5m2": (ml_dtypes.float8_e5m2, 14)}[fmt]
    v = np.moveaxis(np.asarray(x, np.float32).astype(ml_dtypes.bfloat16).astype(np.float64), axis, -1)
    blocks = v.reshape(v.shape[:-1] + (-1, 32))
    amax = np.abs(blocks).max(-1, keepdims=True)
    byte = np.maximum(np.where(amax > 0, np.frexp(amax)[1] - 1 + 127, 0) - down, 1)
    scale = np.exp2(byte - 127.0)
    codes = (blocks / scale).astype(np.float32).astype(dtype).astype(np.float64)
    return np.moveaxis((codes * scale).reshape(v.shape), -1, axis)


WIDE = False


def mx_kscale(k):
    if not WIDE:
        return np.ones(k)
    levels = np.array([10, -10, 5, -5, 0])
    if k % 512:
        return np.exp2(np.random.permutation(np.resize(levels, k // 32))).repeat(32)
    a = np.empty((k // 512, 16))
    for p in range(k // 512):
        a[p, :8] = np.random.permutation(np.resize(levels, 8))
        for g in range(8):
            far = levels[np.abs(levels - a[p, g]) >= 10]
            a[p, g + 8] = far[np.random.randint(len(far))]
    return np.exp2(a.ravel()).repeat(32)


def f64(x):
    return np.asarray(x).astype(np.float64)


def striped(idx):
    return np.tile(idx.reshape(-1, 16).T, (8, 1)).astype(np.uint16)


def unstriped(offs):
    return offs[:16].T.reshape(-1).astype(np.int64)


def striped8(idx):
    return np.concatenate([x.reshape(-1, 16).T for x in idx]).astype(np.uint16)


def runs(offs, k):
    lists = np.stack([offs[16 * r : 16 * r + 16].T.reshape(-1) for r in range(8)]).astype(np.int64)
    return lists[np.arange(k) % 512 // 64]


def pack_weight(w):
    k, n = w.shape
    w = f64(np.asarray(w, np.float32).astype(ml_dtypes.bfloat16)).reshape(k // 32, 32, n)
    amax = np.abs(w).max(1)
    byte = np.clip(np.where(amax > 0, np.frexp(amax)[1] - 1 + 127 - 7, 1), 1, 254)
    scaled = (w * np.exp2(127.0 - byte)[:, None, :]).reshape(k, n).astype(np.float32)
    words = np.ascontiguousarray(scaled.reshape(k // 512, 128, 4, n).transpose(0, 1, 3, 2)).astype(ml_dtypes.float8_e4m3fn).view(np.uint8)
    return words, np.ascontiguousarray(byte.astype(np.uint8).reshape(k // 512, 16, n))


def unpack_weight(words, scales):
    g, p, n, _ = words.shape
    vals = np.ascontiguousarray(words).view(ml_dtypes.float8_e4m3fn).astype(np.float64) * np.repeat(np.exp2(scales.astype(np.float64) - 127.0), 8, axis=1)[..., None]
    return vals.transpose(0, 1, 3, 2).reshape(g * 512, n)


def sigmoid(v):
    return 1.0 / (1.0 + np.exp(-np.maximum(v, -700.0)))

def planes(y):
    n, m = y.shape
    v = y.astype(np.float32).astype(ml_dtypes.bfloat16).astype(np.float64).reshape(n // 32, 32, m)
    top = np.abs(v).max(1)
    byte = np.clip(np.where(top > 0, np.frexp(top)[1] - 1 + 127 - 7, 1), 1, 254)
    codes = (v * np.exp2(127.0 - byte)[:, None, :]).reshape(n, m).astype(np.float32).astype(ml_dtypes.float8_e4m3fn).view(np.uint8)
    words = codes.reshape(n // 512, 128, 4, m).transpose(0, 1, 3, 2)
    return np.ascontiguousarray(words), np.ascontiguousarray(byte.astype(np.uint8).reshape(n // 512, 16, m))


K, T, S, N, H, C = 512, 2048, 512, 512, 512, 512


def setup_inputs():
    n = np.random.standard_normal
    s = mx_kscale(K)[:, None]
    u = mx_kscale(S)
    packed_xT = pack_weight(n((K, T)) * s)
    packed_w1 = pack_weight(n((K, H)) / np.sqrt(K) / s)
    packed_w2 = pack_weight(n((K, H)) / np.sqrt(K) / s)
    packed_w3 = pack_weight(n((H, N)) / np.sqrt(H) / u[:, None])
    return {
        "x_words": packed_xT[0],
        "x_scales": packed_xT[1],
        "w1_words": packed_w1[0],
        "w1_scales": packed_w1[1],
        "w2_words": packed_w2[0],
        "w2_scales": packed_w2[1],
        "tau": np.random.uniform(0.3, 0.9, (H, 1)).astype(np.float32),
        "tau2": np.random.uniform(0.3, 0.9, (H, 1)).astype(np.float32),
        "gn": (np.random.uniform(0.5, 1.5, (H, 1)) * u[:, None]).astype(np.float32),
        "w3_words": packed_w3[0],
        "w3_scales": packed_w3[1],
        "gs": (np.random.uniform(0.5, 1.5, (K, 1)) / s).astype(np.float32),
        "sl": np.random.uniform(1.0, 2.0, (N, 1)).astype(np.float32),
        "th": (0.5 * n((N, 1))).astype(np.float32),
        "sl2": np.random.uniform(1.0, 2.0, (C, 1)).astype(np.float32),
        "th2": (0.5 * n((C, 1))).astype(np.float32),
        "offs": striped(np.random.permutation(T)[:S]),
        "two": striped(np.random.permutation(T)[:S]),
        "n1": striped8(np.stack([np.random.permutation(S) for _ in range(8)])),
        "n2": striped8(np.stack([np.random.permutation(S) for _ in range(8)])),
        "n3": striped(np.random.permutation(S)),
        "n4": striped(np.random.permutation(S)),
        "cand": striped(np.random.permutation(T)[:C]),
        "n5": striped(np.random.permutation(S)),
        "n6": striped(np.random.permutation(S)),
    }


def reference(x_words, x_scales, w1_words, w1_scales, w2_words, w2_scales, tau, tau2, gn, w3_words, w3_scales, gs, sl, th, sl2, th2, offs, two, n1, n2, n3, n4, cand, n5, n6):
    xq = unpack_weight(x_words, x_scales)[:, unstriped(offs)]
    y = unpack_weight(w1_words, w1_scales).T @ xq
    st = np.maximum(y, y[np.arange(H)[:, None], runs(n1, H)])
    z = f64(gn) * (np.minimum(st, st[np.arange(H)[:, None], runs(n2, H)]))
    a = unpack_weight(w3_words, w3_scales).T @ mxq(z, 0, "e4m3")
    sg = sigmoid(f64(sl) * (a[:, unstriped(n5)] - f64(th)))
    x_cand = unpack_weight(x_words, x_scales)[:, unstriped(cand)]
    x_two = unpack_weight(x_words, x_scales)[:, unstriped(two)]
    d = unpack_weight(w2_words, w2_scales).T @ x_two
    top = d.max(axis=1, keepdims=True)
    ea = np.exp(f64(tau) * (d[:, unstriped(n3)] - top))
    ea2 = np.exp(f64(tau2) * (d[:, unstriped(n4)] - top))
    z2 = f64(gs) * (0.5 * d + np.log((ea + 0.25) / (ea2 + 0.25)))
    b = 0.0625 * ((x_cand.T @ mxq(z2, 0, "e4m3")))
    sg2 = sigmoid(f64(sl2) * (b[:, unstriped(n6)] - f64(th2)))
    out_0 = sg * b + sg2 * a
    return (out_0,) + planes(out_0)

@@ -1,0 +1,283 @@
+from contextlib import ExitStack
+
+import concourse.mybir as mybir
+
+F32 = mybir.dt.float32
+BF16 = mybir.dt.bfloat16
+I32 = mybir.dt.int32
+U32 = mybir.dt.uint32
+U16 = mybir.dt.uint16
+U8 = mybir.dt.uint8
+FP8X4 = mybir.dt.float8_e4m3fn_x4
+ALU = mybir.AluOpType
+ACT = mybir.ActivationFunctionType
+
+P = 128
+PACK = 4
+T = 2048
+S = 512
+HALF = S // 2
+FLOPS = 4 * 2 * 512 * 512 * 512
+
+
+def tile_picked_tfcdcxbhopmneos_none_po_kernel(
+    tc, x_words, x_scales, w1_words, w1_scales, w2_words, w2_scales, tau, tau2, gn, w3_words, w3_scales,
+    gs, sl, th, sl2, th2, offs, two, n1, n2, n3, n4, cand, n5, n6, out_0, out_1, out_2,
+):
+    nc = tc.nc
+    with ExitStack() as ctx:
+        keep = ctx.enter_context(tc.tile_pool(name="keep", bufs=1))
+        psum = ctx.enter_context(tc.psum_pool(name="psum", bufs=1))
+
+        def tile(name, shape, dtype):
+            return keep.tile(shape, dtype, name=name, align_bytes=64)
+
+        def load_list(name, src):
+            dst = tile(name, [P, S // 16], U16)
+            nc.sync.dma_start(dst[:], src)
+            return dst
+
+        def load_words(queue, name, src):
+            dst = tile(name, [P, src.shape[2]], U32)
+            queue.dma_start(dst[:].bitcast(I32), src[0].rearrange("p n r -> p (n r)").bitcast(I32))
+            return dst
+
+        def zeroed_plane(engine, name, width):
+            dst = tile(name, [P, width], U8)
+            engine.memset(dst[:].bitcast(I32), 0)
+            return dst
+
+        def load_scales(dst, src):
+            for q in range(4):
+                nc.sync.dma_start(dst[32 * q : 32 * q + 4, :].bitcast(I32), src[0, 4 * q : 4 * q + 4, :].bitcast(I32))
+
+        def load_rows(dst, src):
+            nc.sync.dma_start(dst, src.rearrange("(p t) o -> p (t o)", t=PACK))
+
+        def deal_words(copy, name, src):
+            dst = tile(name, [P, S], U32)
+            copy(dst[:].rearrange("p (t c i) -> p c t i", t=PACK, i=4), src[:].rearrange("p (c i t) -> p c t i", t=PACK, i=4))
+            return dst
+
+        def deal_bytes(copy, name, src):
+            dst = tile(name, [P, S], U8)
+            copy(dst[:].rearrange("p (t m) -> p t m", t=PACK), src[:].rearrange("p (m t) -> p t m", t=PACK))
+            return dst
+
+        def gather(name, dtype, window, offsets):
+            dst = tile(name, [P, S], dtype)
+            nc.vector.tensor_copy(dst[:], window[:].indirect(offsets[:]))
+            return dst
+
+        def product(bank, lhs_words, lhs_bytes, t, rhs_words, rhs_bytes):
+            cols = slice(t * P, (t + 1) * P)
+            nc.tensor.matmul_mx(
+                out=bank, lhsT=lhs_words[:, cols].bitcast(FP8X4), lhsT_scale=lhs_bytes[:, cols],
+                rhs=rhs_words.bitcast(FP8X4), rhs_scale=rhs_bytes, start=True, stop=True,
+            )
+
+        def planar(src, cols):
+            return src[:, :, cols].rearrange("p t (c i) -> p c t i", i=4)
+
+        def woven(dst):
+            return dst.rearrange("p (c i t) -> p c t i", t=PACK, i=4)
+
+        halves = [slice(0, HALF), slice(HALF, S)]
+        low, high = slice(0, S), slice(S, 2 * S)
+
+        w2s_raw = zeroed_plane(nc.vector, "w2s_raw", S)
+        xs = zeroed_plane(nc.gpsimd, "xs", T)
+        w1s_raw = zeroed_plane(nc.vector, "w1s_raw", S)
+        w3s_raw = zeroed_plane(nc.vector, "w3s_raw", S)
+        xw = load_words(nc.scalar, "xw", x_words)
+        l_two = load_list("l_two", two)
+        w2w_raw = load_words(nc.sync, "w2w_raw", w2_words)
+        load_scales(w2s_raw, w2_scales)
+        load_scales(xs, x_scales)
+        taus = tile("taus", [P, 2, 8], F32)
+        load_rows(taus[:, 0, 0:PACK], tau)
+        load_rows(taus[:, 1, 0:PACK], tau2)
+        l_n3 = load_list("l_n3", n3)
+        l_n4 = load_list("l_n4", n4)
+        gs_sb = tile("gs_sb", [P, PACK], F32)
+        load_rows(gs_sb[:], gs)
+        l_offs = load_list("l_offs", offs)
+        w1w_raw = load_words(nc.sync, "w1w_raw", w1_words)
+        load_scales(w1s_raw, w1_scales)
+        l_cand = load_list("l_cand", cand)
+        l_n1 = load_list("l_n1", n1)
+        l_n2 = load_list("l_n2", n2)
+        gn_sb = tile("gn_sb", [P, PACK], F32)
+        load_rows(gn_sb[:], gn)
+        w3w_raw = load_words(nc.sync, "w3w_raw", w3_words)
+        load_scales(w3s_raw, w3_scales)
+        slopes = tile("slopes", [P, 2, 8], F32)
+        load_rows(slopes[:, 0, 0:PACK], sl)
+        load_rows(slopes[:, 1, 0:PACK], sl2)
+        ths = tile("ths", [P, 2, 8], F32)
+        load_rows(ths[:, 0, 0:PACK], th)
+        load_rows(ths[:, 1, 0:PACK], th2)
+        l_n6 = load_list("l_n6", n6)
+        l_n5 = load_list("l_n5", n5)
+
+        def windows(name):
+            return [tile("%s%d" % (name, t), [P, 2 * S], F32) for t in range(PACK)]
+
+        d_win, y_win, st_win, a_win, b_win = windows("d"), windows("y"), windows("st"), windows("a"), windows("b")
+        for win in d_win + y_win:
+            nc.vector.memset(win[:, high], 0.0)
+
+        w2w = deal_words(nc.scalar.copy, "w2w", w2w_raw)
+        w2s = deal_bytes(nc.vector.tensor_copy, "w2s", w2s_raw)
+        two_w = gather("two_w", U32, xw, l_two)
+        two_s = gather("two_s", U8, xs, l_two)
+        neg_taus = tile("neg_taus", [P, 2, PACK], F32)
+        nc.scalar.activation(neg_taus[:], taus[:, :, 0:PACK], ACT.Copy, scale=-1.0)
+        w1w = deal_words(nc.scalar.copy, "w1w", w1w_raw)
+        w1s = deal_bytes(nc.gpsimd.tensor_copy, "w1s", w1s_raw)
+        half_gs = tile("half_gs", [P, PACK], F32)
+        nc.gpsimd.tensor_scalar(half_gs[:], gs_sb[:], 0.5, 0.0, ALU.mult, ALU.add)
+
+        d_ps = [psum.tile([P, S], F32, name="d_ps%d" % t, tag="left%d" % t) for t in range(PACK)]
+        y_ps = [psum.tile([P, S], F32, name="y_ps%d" % t, tag="right%d" % t) for t in range(PACK)]
+        for t in range(PACK):
+            product(d_ps[t][:], w2w, w2s, t, two_w[:], two_s[:])
+        top = tile("top", [P, PACK], F32)
+
+        def empty_d(t):
+            nc.vector.tensor_scalar(d_win[t][:, low], d_ps[t][:], 1.0, None, ALU.mult, ALU.max, accum_out=top[:, t : t + 1])
+            nc.gpsimd.tensor_scalar(b_win[t][:, high], d_win[t][:, low], half_gs[:, t : t + 1], 0.0, ALU.mult, ALU.add)
+
+        offs_w = gather("offs_w", U32, xw, l_offs)
+        empty_d(0)
+        offs_s = gather("offs_s", U8, xs, l_offs)
+        for t in range(PACK):
+            product(y_ps[t][:], w1w, w1s, t, offs_w[:], offs_s[:])
+        for t in range(1, PACK):
+            empty_d(t)
+        cand_w = deal_words(nc.vector.tensor_copy, "cand_w", gather("cand_w_raw", U32, xw, l_cand))
+        cand_s = deal_bytes(nc.vector.tensor_copy, "cand_s", gather("cand_s_raw", U8, xs, l_cand))
+
+        Y_ON_S, N1_ON_S, N2_ON_S, A_ON_S, B_ON_S = (2,3), (), (0,1,2,3), (4,5,6,7), (0,1,2,3)
+        sub_engine = nc.vector
+        add_engine = nc.vector
+
+        def fetch(on_scalar, dst, win, lst):
+            if on_scalar:
+                nc.scalar.activation(dst, win[:].indirect(lst[:]), ACT.Copy)
+            else:
+                nc.vector.tensor_copy(dst, win[:].indirect(lst[:]))
+
+        exp_bias = tile("exp_bias", [P, PACK, 2], F32)
+        e = tile("e", [P, PACK, 2, S], F32)
+        for t in range(PACK):
+            nc.scalar.activation(exp_bias[:, t, :], neg_taus[:, :, t], ACT.Copy, scale=top[:, t : t + 1])
+            for k, lst in enumerate((l_n3, l_n4)):
+                nc.scalar.activation(
+                    e[:, t, k, :], d_win[t][:].indirect(lst[:]), ACT.Exp,
+                    bias=exp_bias[:, t, k : k + 1], scale=taus[:, k, t : t + 1],
+                )
+            if t in Y_ON_S:
+                nc.scalar.copy(y_win[t][:, low], y_ps[t][:])
+            else:
+                nc.vector.tensor_copy(y_win[t][:, low], y_ps[t][:])
+            if t in N1_ON_S:
+                fetch(True, st_win[t][:, high], y_win[t], l_n1)
+        w3s = deal_bytes(nc.gpsimd.tensor_copy, "w3s", w3s_raw)
+
+        for t in range(PACK):
+            if t not in N1_ON_S:
+                fetch(False, st_win[t][:, high], y_win[t], l_n1)
+            nc.vector.tensor_tensor(st_win[t][:, low], st_win[t][:, high], y_ps[t][:], ALU.max)
+        sig_bias = tile("sig_bias", [P, 2, PACK], F32)
+        nc.vector.scalar_tensor_tensor(sig_bias[:], slopes[:, :, 0:PACK], -1.0, ths[:, :, 0:PACK], ALU.mult, ALU.mult)
+
+        diff = tile("diff", [P, PACK, S], F32)
+        z2_rows = tile("z2_rows", [P, PACK, S], BF16)
+        def half_banks(name, tag):
+            banks = [psum.tile([P, 2, HALF], F32, name="%s%d" % (name, k), tag="%s%d" % (tag, k)) for k in range(PACK)]
+            return banks, [[banks[2 * h + t // 2][:, t % 2, :] for t in range(PACK)] for h in range(2)]
+
+        b_banks, b_ps = half_banks("b_ps", "left")
+        for h in range(2):
+            nc.scalar.activation(e[:, :, :, halves[h]], e[:, :, :, halves[h]], ACT.Ln, bias=0.25)
+        for h in range(2):
+            cols = halves[h]
+            for u in range(0, PACK, 4):
+                sub_engine.tensor_tensor(diff[:, u : u + 4, cols], e[:, u : u + 4, 0, cols], e[:, u : u + 4, 1, cols], ALU.subtract)
+            for t in range(PACK):
+                nc.vector.scalar_tensor_tensor(
+                    z2_rows[:, t, cols], diff[:, t, cols], gs_sb[:, t : t + 1], b_win[t][:, high][:, cols], ALU.mult, ALU.add
+                )
+            z2_in = tile("z2_in%d" % h, [P, HALF * PACK], BF16)
+            z2_w = tile("z2_w%d" % h, [P, HALF], U32)
+            z2_s = tile("z2_s%d" % h, [P, HALF], U8)
+            nc.vector.tensor_copy(woven(z2_in[:]), planar(z2_rows, cols))
+            nc.vector.quantize_mx(z2_w[:].bitcast(FP8X4), z2_s[:], z2_in[:])
+            for t in range(PACK):
+                product(b_ps[h][t], cand_w, cand_s, t, z2_w[:], z2_s[:])
+        for t in range(PACK):
+            fetch(t in N2_ON_S, a_win[t][:, high], st_win[t], l_n2)
+        w3w = deal_words(nc.scalar.copy, "w3w", w3w_raw)
+        sg2 = tile("sg2", [P, PACK, S], F32)
+        for h in range(2):
+            for t in range(PACK):
+                if 4 * h + t in B_ON_S:
+                    nc.scalar.activation(b_win[t][:, halves[h]], b_ps[h][t], ACT.Copy, scale=0.0625)
+                else:
+                    nc.vector.tensor_scalar(b_win[t][:, halves[h]], b_ps[h][t], 0.0625, None, ALU.mult)
+        for t in range(PACK):
+            nc.scalar.activation(
+                sg2[:, t, :], b_win[t][:].indirect(l_n6[:]), ACT.Sigmoid,
+                bias=sig_bias[:, 1, t : t + 1], scale=slopes[:, 1, t : t + 1],
+            )
+
+        least = diff
+        for t in range(PACK):
+            nc.vector.tensor_tensor(least[:, t, :], st_win[t][:, low], a_win[t][:, high], ALU.min)
+        a_banks, a_ps = half_banks("a_ps", "right")
+        gn_view = gn_sb[:].unsqueeze(1).unsqueeze(3).to_broadcast([P, HALF // 4, PACK, 4])
+        z_in = [tile("z_in%d" % h, [P, HALF * PACK], BF16) for h in range(2)]
+        z_w = [tile("z_w%d" % h, [P, HALF], U32) for h in range(2)]
+        z_s = [tile("z_s%d" % h, [P, HALF], U8) for h in range(2)]
+        for h in range(2):
+            nc.vector.tensor_tensor(woven(z_in[h][:]), planar(least, halves[h]), gn_view, ALU.mult)
+        for h in range(2):
+            nc.vector.quantize_mx(z_w[h][:].bitcast(FP8X4), z_s[h][:], z_in[h][:])
+            for t in range(PACK):
+                product(a_ps[h][t], w3w, w3s, t, z_w[h][:], z_s[h][:])
+
+        sg = tile("sg", [P, PACK, S], F32)
+        p1 = tile("p1", [P, PACK, S], F32)
+        p2 = tile("p2", [P, PACK, S], F32)
+        res = tile("res", [P, PACK, S], F32)
+        for h in range(2):
+            for t in range(PACK):
+                if 4 * h + t in A_ON_S:
+                    nc.scalar.copy(a_win[t][:, halves[h]], a_ps[h][t])
+                else:
+                    nc.vector.tensor_copy(a_win[t][:, halves[h]], a_ps[h][t])
+        for h in range(2):
+            for u in range(2):
+                nc.vector.tensor_tensor(p2[:, 2 * u : 2 * u + 2, halves[h]], sg2[:, 2 * u : 2 * u + 2, halves[h]], a_banks[2 * h + u][:], ALU.mult)
+        out_rows = out_0.rearrange("(p t) j -> p t j", t=PACK)
+        out_words = out_1[0].rearrange("p n r -> p (n r)").bitcast(I32)
+        res_in = [tile("res_in%d" % h, [P, HALF * PACK], BF16) for h in range(2)]
+        res_w = tile("res_w", [P, S], U32)
+        res_s = tile("res_s", [P, S], U8)
+        for h in range(2):
+            cols = halves[h]
+            for t in range(PACK):
+                nc.scalar.activation(
+                    sg[:, t, cols], a_win[t][:].indirect(l_n5[:, h * 16 : (h + 1) * 16]), ACT.Sigmoid,
+                    bias=sig_bias[:, 0, t : t + 1], scale=slopes[:, 0, t : t + 1],
+                )
+                nc.vector.scalar_tensor_tensor(p1[:, t, cols], b_ps[h][t], 0.0625, sg[:, t, cols], ALU.mult, ALU.mult)
+                add_engine.tensor_tensor(res[:, t, cols], p1[:, t, cols], p2[:, t, cols], ALU.add)
+                nc.sync.dma_start(out_rows[:, t, cols], res[:, t, cols])
+            nc.vector.tensor_copy(woven(res_in[h][:]), planar(res, cols))
+            nc.vector.quantize_mx(res_w[:, cols].bitcast(FP8X4), res_s[:, cols], res_in[h][:])
+            nc.sync.dma_start(out_words[:, cols], res_w[:, cols].bitcast(I32))
+        for q in range(4):
+            queue = nc.scalar if q % 2 == 0 else nc.sync
+            queue.dma_start(out_2[0, 4 * q : 4 * q + 4, :].bitcast(I32), res_s[32 * q : 32 * q + 4, :].bitcast(I32))

@@ -29,8 +29,8 @@ def tile_picked_tfcdcxbhopmneos_none_po_kernel(
         keep = ctx.enter_context(tc.tile_pool(name="keep", bufs=1))
         psum = ctx.enter_context(tc.psum_pool(name="psum", bufs=1))
 
-        def tile(name, shape, dtype):
-            return keep.tile(shape, dtype, name=name, align_bytes=64)
+        def tile(name, shape, dtype, tag=None):
+            return keep.tile(shape, dtype, name=name, tag=tag or name, align_bytes=64)
 
         def load_list(name, src):
             dst = tile(name, [P, S // 16], U16)
@@ -51,21 +51,21 @@ def tile_picked_tfcdcxbhopmneos_none_po_kernel(
             for q in range(4):
                 nc.sync.dma_start(dst[32 * q : 32 * q + 4, :].bitcast(I32), src[0, 4 * q : 4 * q + 4, :].bitcast(I32))
 
-        def load_rows(dst, src):
-            nc.sync.dma_start(dst, src.rearrange("(p t) o -> p (t o)", t=PACK))
+        def load_rows(dst, src, queue=nc.sync):
+            queue.dma_start(dst, src.rearrange("(p t) o -> p (t o)", t=PACK))
 
-        def deal_words(copy, name, src):
-            dst = tile(name, [P, S], U32)
+        def deal_words(copy, name, src, tag=None):
+            dst = tile(name, [P, S], U32, tag)
             copy(dst[:].rearrange("p (t c i) -> p c t i", t=PACK, i=4), src[:].rearrange("p (c i t) -> p c t i", t=PACK, i=4))
             return dst
 
-        def deal_bytes(copy, name, src):
-            dst = tile(name, [P, S], U8)
+        def deal_bytes(copy, name, src, tag=None):
+            dst = tile(name, [P, S], U8, tag)
             copy(dst[:].rearrange("p (t m) -> p t m", t=PACK), src[:].rearrange("p (m t) -> p t m", t=PACK))
             return dst
 
-        def gather(name, dtype, window, offsets):
-            dst = tile(name, [P, S], dtype)
+        def gather(name, dtype, window, offsets, tag=None):
+            dst = tile(name, [P, S], dtype, tag)
             nc.vector.tensor_copy(dst[:], window[:].indirect(offsets[:]))
             return dst
 
@@ -85,19 +85,19 @@ def tile_picked_tfcdcxbhopmneos_none_po_kernel(
         halves = [slice(0, HALF), slice(HALF, S)]
         low, high = slice(0, S), slice(S, 2 * S)
 
-        w2s_raw = zeroed_plane(nc.vector, "w2s_raw", S)
         xs = zeroed_plane(nc.gpsimd, "xs", T)
+        w2s_raw = zeroed_plane(nc.gpsimd, "w2s_raw", S)
         w1s_raw = zeroed_plane(nc.vector, "w1s_raw", S)
         w3s_raw = zeroed_plane(nc.vector, "w3s_raw", S)
+        taus = tile("taus", [P, 2, 8], F32)
+        load_rows(taus[:, 0, 0:PACK], tau, nc.scalar)
+        load_rows(taus[:, 1, 0:PACK], tau2, nc.scalar)
         xw = load_words(nc.scalar, "xw", x_words)
         l_two = load_list("l_two", two)
-        w2w_raw = load_words(nc.sync, "w2w_raw", w2_words)
-        load_scales(w2s_raw, w2_scales)
         load_scales(xs, x_scales)
-        taus = tile("taus", [P, 2, 8], F32)
-        load_rows(taus[:, 0, 0:PACK], tau)
-        load_rows(taus[:, 1, 0:PACK], tau2)
+        load_scales(w2s_raw, w2_scales)
         l_n3 = load_list("l_n3", n3)
+        w2w_raw = load_words(nc.sync, "w2w_raw", w2_words)
         l_n4 = load_list("l_n4", n4)
         gs_sb = tile("gs_sb", [P, PACK], F32)
         load_rows(gs_sb[:], gs)
@@ -120,10 +120,11 @@ def tile_picked_tfcdcxbhopmneos_none_po_kernel(
         l_n6 = load_list("l_n6", n6)
         l_n5 = load_list("l_n5", n5)
 
-        def windows(name):
-            return [tile("%s%d" % (name, t), [P, 2 * S], F32) for t in range(PACK)]
+        def windows(name, width=2 * S):
+            return [tile("%s%d" % (name, t), [P, width], F32) for t in range(PACK)]
 
-        d_win, y_win, st_win, a_win, b_win = windows("d"), windows("y"), windows("st"), windows("a"), windows("b")
+        d_win, y_win, st_win, a_win, b_win = windows("d"), windows("y"), windows("st"), windows("a", S), windows("b")
+        st_far = tile("st_far", [P, PACK, S], F32)
         for win in d_win + y_win:
             nc.vector.memset(win[:, high], 0.0)
 
@@ -150,15 +151,15 @@ def tile_picked_tfcdcxbhopmneos_none_po_kernel(
 
         offs_w = gather("offs_w", U32, xw, l_offs)
         empty_d(0)
-        offs_s = gather("offs_s", U8, xs, l_offs)
+        offs_s = gather("offs_s", U8, xs, l_offs, "two_s")
         for t in range(PACK):
             product(y_ps[t][:], w1w, w1s, t, offs_w[:], offs_s[:])
         for t in range(1, PACK):
             empty_d(t)
-        cand_w = deal_words(nc.vector.tensor_copy, "cand_w", gather("cand_w_raw", U32, xw, l_cand))
-        cand_s = deal_bytes(nc.vector.tensor_copy, "cand_s", gather("cand_s_raw", U8, xs, l_cand))
+        cand_w = deal_words(nc.vector.tensor_copy, "cand_w", gather("cand_w_raw", U32, xw, l_cand), "w1w")
+        cand_s = deal_bytes(nc.vector.tensor_copy, "cand_s", gather("cand_s_raw", U8, xs, l_cand), "w1s")
 
-        Y_ON_S, N1_ON_S, N2_ON_S, A_ON_S, B_ON_S = (2,3), (), (0,1,2,3), (4,5,6,7), (0,1,2,3)
+        Y_ON_S, N1_ON_S, N2_ON_S, A_ON_S, B_ON_S = (2,3), (), (0,1,2,3), (), (0,1,2,3)
         sub_engine = nc.vector
         add_engine = nc.vector
 
@@ -204,7 +205,7 @@ def tile_picked_tfcdcxbhopmneos_none_po_kernel(
         for h in range(2):
             cols = halves[h]
             for u in range(0, PACK, 4):
-                sub_engine.tensor_tensor(diff[:, u : u + 4, cols], e[:, u : u + 4, 0, cols], e[:, u : u + 4, 1, cols], ALU.subtract)
+                (nc.gpsimd if h in () else nc.vector).tensor_tensor(diff[:, u : u + 4, cols], e[:, u : u + 4, 0, cols], e[:, u : u + 4, 1, cols], ALU.subtract)
             for t in range(PACK):
                 nc.vector.scalar_tensor_tensor(
                     z2_rows[:, t, cols], diff[:, t, cols], gs_sb[:, t : t + 1], b_win[t][:, high][:, cols], ALU.mult, ALU.add
@@ -217,8 +218,8 @@ def tile_picked_tfcdcxbhopmneos_none_po_kernel(
             for t in range(PACK):
                 product(b_ps[h][t], cand_w, cand_s, t, z2_w[:], z2_s[:])
         for t in range(PACK):
-            fetch(t in N2_ON_S, a_win[t][:, high], st_win[t], l_n2)
-        w3w = deal_words(nc.scalar.copy, "w3w", w3w_raw)
+            fetch(t in N2_ON_S, st_far[:, t, :], st_win[t], l_n2)
+        w3w = deal_words(nc.gpsimd.tensor_copy, "w3w", w3w_raw)
         sg2 = tile("sg2", [P, PACK, S], F32)
         for h in range(2):
             for t in range(PACK):
@@ -234,18 +235,17 @@ def tile_picked_tfcdcxbhopmneos_none_po_kernel(
 
         least = diff
         for t in range(PACK):
-            nc.vector.tensor_tensor(least[:, t, :], st_win[t][:, low], a_win[t][:, high], ALU.min)
+            nc.vector.tensor_tensor(least[:, t, :], st_win[t][:, low], st_far[:, t, :], ALU.min)
         a_banks, a_ps = half_banks("a_ps", "right")
         gn_view = gn_sb[:].unsqueeze(1).unsqueeze(3).to_broadcast([P, HALF // 4, PACK, 4])
-        z_in = [tile("z_in%d" % h, [P, HALF * PACK], BF16) for h in range(2)]
-        z_w = [tile("z_w%d" % h, [P, HALF], U32) for h in range(2)]
-        z_s = [tile("z_s%d" % h, [P, HALF], U8) for h in range(2)]
         for h in range(2):
-            nc.vector.tensor_tensor(woven(z_in[h][:]), planar(least, halves[h]), gn_view, ALU.mult)
-        for h in range(2):
-            nc.vector.quantize_mx(z_w[h][:].bitcast(FP8X4), z_s[h][:], z_in[h][:])
+            z_in = tile("z_in%d" % h, [P, HALF * PACK], BF16, "z_in")
+            z_w = tile("z_w%d" % h, [P, HALF], U32)
+            z_s = tile("z_s%d" % h, [P, HALF], U8)
+            nc.vector.tensor_tensor(woven(z_in[:]), planar(least, halves[h]), gn_view, ALU.mult)
+            nc.vector.quantize_mx(z_w[:].bitcast(FP8X4), z_s[:], z_in[:])
             for t in range(PACK):
-                product(a_ps[h][t], w3w, w3s, t, z_w[h][:], z_s[h][:])
+                product(a_ps[h][t], w3w, w3s, t, z_w[:], z_s[:])
 
         sg = tile("sg", [P, PACK, S], F32)
         p1 = tile("p1", [P, PACK, S], F32)
@@ -259,24 +259,34 @@ def tile_picked_tfcdcxbhopmneos_none_po_kernel(
                     nc.vector.tensor_copy(a_win[t][:, halves[h]], a_ps[h][t])
         for h in range(2):
             for u in range(2):
+                if 2 * h + u in (0,1):
+                    for t in (2 * u, 2 * u + 1):
+                        nc.gpsimd.tensor_tensor(p2[:, t, halves[h]], sg2[:, t, halves[h]], a_win[t][:, halves[h]], ALU.mult)
+                    continue
                 nc.vector.tensor_tensor(p2[:, 2 * u : 2 * u + 2, halves[h]], sg2[:, 2 * u : 2 * u + 2, halves[h]], a_banks[2 * h + u][:], ALU.mult)
         out_rows = out_0.rearrange("(p t) j -> p t j", t=PACK)
         out_words = out_1[0].rearrange("p n r -> p (n r)").bitcast(I32)
-        res_in = [tile("res_in%d" % h, [P, HALF * PACK], BF16) for h in range(2)]
         res_w = tile("res_w", [P, S], U32)
         res_s = tile("res_s", [P, S], U8)
-        for h in range(2):
-            cols = halves[h]
+        for c, (first, last, group, adder, weaver) in enumerate([(0, 256, 2, nc.vector, nc.scalar.copy), (256, 512, 2, nc.vector, nc.vector.tensor_copy)]):
+            cols, h = slice(first, last), first // HALF
+            part = slice(first - h * HALF, last - h * HALF)
             for t in range(PACK):
                 nc.scalar.activation(
-                    sg[:, t, cols], a_win[t][:].indirect(l_n5[:, h * 16 : (h + 1) * 16]), ACT.Sigmoid,
+                    sg[:, t, cols], a_win[t][:].indirect(l_n5[:, first // 16 : last // 16]), ACT.Sigmoid,
                     bias=sig_bias[:, 0, t : t + 1], scale=slopes[:, 0, t : t + 1],
                 )
-                nc.vector.scalar_tensor_tensor(p1[:, t, cols], b_ps[h][t], 0.0625, sg[:, t, cols], ALU.mult, ALU.mult)
-                add_engine.tensor_tensor(res[:, t, cols], p1[:, t, cols], p2[:, t, cols], ALU.add)
-                nc.sync.dma_start(out_rows[:, t, cols], res[:, t, cols])
-            nc.vector.tensor_copy(woven(res_in[h][:]), planar(res, cols))
-            nc.vector.quantize_mx(res_w[:, cols].bitcast(FP8X4), res_s[:, cols], res_in[h][:])
+                if (t + 1) % group:
+                    continue
+                rows = slice(t + 1 - group, t + 1)
+                b_part = b_banks[2 * h + t // 2][:, slice(t % 2 + 1 - group, t % 2 + 1), part]
+                nc.vector.scalar_tensor_tensor(p1[:, rows, cols], b_part, 0.0625, sg[:, rows, cols], ALU.mult, ALU.mult)
+                adder.tensor_tensor(res[:, rows, cols], p1[:, rows, cols], p2[:, rows, cols], ALU.add)
+                if t % 2:
+                    nc.sync.dma_start(out_rows[:, t - 1 : t + 1, cols], res[:, t - 1 : t + 1, cols])
+            res_in = tile("res_in%d" % c, [P, (last - first) * PACK], BF16)
+            weaver(woven(res_in[:]), planar(res, cols))
+            nc.vector.quantize_mx(res_w[:, cols].bitcast(FP8X4), res_s[:, cols], res_in[:])
             nc.sync.dma_start(out_words[:, cols], res_w[:, cols].bitcast(I32))
         for q in range(4):
             queue = nc.scalar if q % 2 == 0 else nc.sync

@@ -54,13 +54,13 @@ def tile_picked_tfcdcxbhopmneos_none_po_kernel(
         def load_rows(dst, src, queue=nc.sync):
             queue.dma_start(dst, src.rearrange("(p t) o -> p (t o)", t=PACK))
 
-        def deal_words(copy, name, src, tag=None):
-            dst = tile(name, [P, S], U32, tag)
+        def deal_words(copy, name, src):
+            dst = tile(name, [P, S], U32)
             copy(dst[:].rearrange("p (t c i) -> p c t i", t=PACK, i=4), src[:].rearrange("p (c i t) -> p c t i", t=PACK, i=4))
             return dst
 
-        def deal_bytes(copy, name, src, tag=None):
-            dst = tile(name, [P, S], U8, tag)
+        def deal_bytes(copy, name, src):
+            dst = tile(name, [P, S], U8)
             copy(dst[:].rearrange("p (t m) -> p t m", t=PACK), src[:].rearrange("p (m t) -> p t m", t=PACK))
             return dst
 
@@ -135,9 +135,9 @@ def tile_picked_tfcdcxbhopmneos_none_po_kernel(
         neg_taus = tile("neg_taus", [P, 2, PACK], F32)
         nc.scalar.activation(neg_taus[:], taus[:, :, 0:PACK], ACT.Copy, scale=-1.0)
         w1w = deal_words(nc.scalar.copy, "w1w", w1w_raw)
-        w1s = deal_bytes(nc.gpsimd.tensor_copy, "w1s", w1s_raw)
+        w1s = deal_bytes(nc.vector.tensor_copy, "w1s", w1s_raw)
         half_gs = tile("half_gs", [P, PACK], F32)
-        nc.gpsimd.tensor_scalar(half_gs[:], gs_sb[:], 0.5, 0.0, ALU.mult, ALU.add)
+        nc.vector.tensor_scalar(half_gs[:], gs_sb[:], 0.5, 0.0, ALU.mult, ALU.add)
 
         d_ps = [psum.tile([P, S], F32, name="d_ps%d" % t, tag="left%d" % t) for t in range(PACK)]
         y_ps = [psum.tile([P, S], F32, name="y_ps%d" % t, tag="right%d" % t) for t in range(PACK)]
@@ -147,7 +147,7 @@ def tile_picked_tfcdcxbhopmneos_none_po_kernel(
 
         def empty_d(t):
             nc.vector.tensor_scalar(d_win[t][:, low], d_ps[t][:], 1.0, None, ALU.mult, ALU.max, accum_out=top[:, t : t + 1])
-            nc.gpsimd.tensor_scalar(b_win[t][:, high], d_win[t][:, low], half_gs[:, t : t + 1], 0.0, ALU.mult, ALU.add)
+            (nc.gpsimd if t in (0,1) else nc.vector).tensor_scalar(b_win[t][:, high], d_win[t][:, low], half_gs[:, t : t + 1], 0.0, ALU.mult, ALU.add)
 
         offs_w = gather("offs_w", U32, xw, l_offs)
         empty_d(0)
@@ -156,8 +156,8 @@ def tile_picked_tfcdcxbhopmneos_none_po_kernel(
             product(y_ps[t][:], w1w, w1s, t, offs_w[:], offs_s[:])
         for t in range(1, PACK):
             empty_d(t)
-        cand_w = deal_words(nc.vector.tensor_copy, "cand_w", gather("cand_w_raw", U32, xw, l_cand), "w1w")
-        cand_s = deal_bytes(nc.vector.tensor_copy, "cand_s", gather("cand_s_raw", U8, xs, l_cand), "w1s")
+        cand_w = deal_words(nc.vector.tensor_copy, "cand_w", gather("cand_w_raw", U32, xw, l_cand))
+        cand_s = deal_bytes(nc.vector.tensor_copy, "cand_s", gather("cand_s_raw", U8, xs, l_cand))
 
         Y_ON_S, N1_ON_S, N2_ON_S, A_ON_S, B_ON_S = (2,3), (), (0,1,2,3), (), (0,1,2,3)
         sub_engine = nc.vector
@@ -184,7 +184,7 @@ def tile_picked_tfcdcxbhopmneos_none_po_kernel(
                 nc.vector.tensor_copy(y_win[t][:, low], y_ps[t][:])
             if t in N1_ON_S:
                 fetch(True, st_win[t][:, high], y_win[t], l_n1)
-        w3s = deal_bytes(nc.gpsimd.tensor_copy, "w3s", w3s_raw)
+        w3s = deal_bytes(nc.vector.tensor_copy, "w3s", w3s_raw)
 
         for t in range(PACK):
             if t not in N1_ON_S:
@@ -213,13 +213,13 @@ def tile_picked_tfcdcxbhopmneos_none_po_kernel(
             z2_in = tile("z2_in%d" % h, [P, HALF * PACK], BF16)
             z2_w = tile("z2_w%d" % h, [P, HALF], U32)
             z2_s = tile("z2_s%d" % h, [P, HALF], U8)
-            nc.vector.tensor_copy(woven(z2_in[:]), planar(z2_rows, cols))
+            (nc.scalar.copy if h in (1,) else nc.vector.tensor_copy)(woven(z2_in[:]), planar(z2_rows, cols))
             nc.vector.quantize_mx(z2_w[:].bitcast(FP8X4), z2_s[:], z2_in[:])
             for t in range(PACK):
                 product(b_ps[h][t], cand_w, cand_s, t, z2_w[:], z2_s[:])
         for t in range(PACK):
             fetch(t in N2_ON_S, st_far[:, t, :], st_win[t], l_n2)
-        w3w = deal_words(nc.gpsimd.tensor_copy, "w3w", w3w_raw)
+        w3w = deal_words(nc.scalar.copy, "w3w", w3w_raw)
         sg2 = tile("sg2", [P, PACK, S], F32)
         for h in range(2):
             for t in range(PACK):

@@ -14,10 +14,14 @@ ACT = mybir.ActivationFunctionType
 
 P = 128
 PACK = 4
+QUADRANTS = 4
 T = 2048
 S = 512
 HALF = S // 2
-FLOPS = 4 * 2 * 512 * 512 * 512
+LINE = 4
+ROW_PITCH = 8
+HALF_D_ON_GPSIMD = 2
+FLOPS = 4 * 2 * S * S * S
 
 
 def tile_picked_tfcdcxbhopmneos_none_po_kernel(
@@ -42,100 +46,113 @@ def tile_picked_tfcdcxbhopmneos_none_po_kernel(
             queue.dma_start(dst[:].bitcast(I32), src[0].rearrange("p n r -> p (n r)").bitcast(I32))
             return dst
 
-        def zeroed_plane(engine, name, width):
+        def zeroed_scale_tile(engine, name, width):
             dst = tile(name, [P, width], U8)
             engine.memset(dst[:].bitcast(I32), 0)
             return dst
 
         def load_scales(dst, src):
-            for q in range(4):
+            for q in range(QUADRANTS):
                 nc.sync.dma_start(dst[32 * q : 32 * q + 4, :].bitcast(I32), src[0, 4 * q : 4 * q + 4, :].bitcast(I32))
 
-        def load_rows(dst, src, queue=nc.sync):
+        def load_rows(queue, dst, src):
             queue.dma_start(dst, src.rearrange("(p t) o -> p (t o)", t=PACK))
 
         def deal_words(copy, name, src):
             dst = tile(name, [P, S], U32)
-            copy(dst[:].rearrange("p (t c i) -> p c t i", t=PACK, i=4), src[:].rearrange("p (c i t) -> p c t i", t=PACK, i=4))
+            copy(
+                dst[:].rearrange("p (t c i) -> p c t i", t=PACK, i=LINE),
+                src[:].rearrange("p (c i t) -> p c t i", t=PACK, i=LINE),
+            )
             return dst
 
-        def deal_bytes(copy, name, src):
+        def deal_bytes(name, src):
             dst = tile(name, [P, S], U8)
-            copy(dst[:].rearrange("p (t m) -> p t m", t=PACK), src[:].rearrange("p (m t) -> p t m", t=PACK))
+            nc.vector.tensor_copy(
+                dst[:].rearrange("p (t m) -> p t m", t=PACK), src[:].rearrange("p (m t) -> p t m", t=PACK)
+            )
             return dst
 
-        def gather(name, dtype, window, offsets, tag=None):
+        def gather_packed(name, dtype, window, offsets, tag=None):
             dst = tile(name, [P, S], dtype, tag)
             nc.vector.tensor_copy(dst[:], window[:].indirect(offsets[:]))
             return dst
 
-        def product(bank, lhs_words, lhs_bytes, t, rhs_words, rhs_bytes):
+        def product(out, lhs_words, lhs_bytes, t, rhs_words, rhs_bytes):
             cols = slice(t * P, (t + 1) * P)
             nc.tensor.matmul_mx(
-                out=bank, lhsT=lhs_words[:, cols].bitcast(FP8X4), lhsT_scale=lhs_bytes[:, cols],
+                out=out, lhsT=lhs_words[:, cols].bitcast(FP8X4), lhsT_scale=lhs_bytes[:, cols],
                 rhs=rhs_words.bitcast(FP8X4), rhs_scale=rhs_bytes, start=True, stop=True,
             )
 
-        def planar(src, cols):
-            return src[:, :, cols].rearrange("p t (c i) -> p c t i", i=4)
+        def row_tiles(src, cols):
+            return src[:, :, cols].rearrange("p t (c i) -> p c t i", i=LINE)
 
         def woven(dst):
-            return dst.rearrange("p (c i t) -> p c t i", t=PACK, i=4)
+            return dst.rearrange("p (c i t) -> p c t i", t=PACK, i=LINE)
+
+        def windows(name, width):
+            return [tile("%s%d" % (name, t), [P, width], F32) for t in range(PACK)]
+
+        def half_banks(name, tag):
+            banks = [psum.tile([P, 2, HALF], F32, name="%s%d" % (name, k), tag="%s%d" % (tag, k)) for k in range(PACK)]
+            return banks, [[banks[2 * h + t // 2][:, t % 2, :] for t in range(PACK)] for h in range(2)]
 
         halves = [slice(0, HALF), slice(HALF, S)]
-        low, high = slice(0, S), slice(S, 2 * S)
+        rows_part, spare_part = slice(0, S), slice(S, 2 * S)
 
-        xs = zeroed_plane(nc.gpsimd, "xs", T)
-        w2s_raw = zeroed_plane(nc.gpsimd, "w2s_raw", S)
-        w1s_raw = zeroed_plane(nc.vector, "w1s_raw", S)
-        w3s_raw = zeroed_plane(nc.vector, "w3s_raw", S)
-        taus = tile("taus", [P, 2, 8], F32)
-        load_rows(taus[:, 0, 0:PACK], tau, nc.scalar)
-        load_rows(taus[:, 1, 0:PACK], tau2, nc.scalar)
+        w2s_raw = zeroed_scale_tile(nc.gpsimd, "w2s_raw", S)
+        xs = zeroed_scale_tile(nc.gpsimd, "xs", T)
+        w1s_raw = zeroed_scale_tile(nc.vector, "w1s_raw", S)
+        w3s_raw = zeroed_scale_tile(nc.vector, "w3s_raw", S)
+        taus = tile("taus", [P, 2, ROW_PITCH], F32)
+        load_rows(nc.scalar, taus[:, 0, 0:PACK], tau)
+        load_rows(nc.scalar, taus[:, 1, 0:PACK], tau2)
         xw = load_words(nc.scalar, "xw", x_words)
         l_two = load_list("l_two", two)
-        load_scales(xs, x_scales)
         load_scales(w2s_raw, w2_scales)
+        load_scales(xs, x_scales)
         l_n3 = load_list("l_n3", n3)
         w2w_raw = load_words(nc.sync, "w2w_raw", w2_words)
+        l_offs = load_list("l_offs", offs)
         l_n4 = load_list("l_n4", n4)
         gs_sb = tile("gs_sb", [P, PACK], F32)
-        load_rows(gs_sb[:], gs)
-        l_offs = load_list("l_offs", offs)
+        load_rows(nc.sync, gs_sb[:], gs)
         w1w_raw = load_words(nc.sync, "w1w_raw", w1_words)
+        w3w_raw = load_words(nc.sync, "w3w_raw", w3_words)
         load_scales(w1s_raw, w1_scales)
         l_cand = load_list("l_cand", cand)
         l_n1 = load_list("l_n1", n1)
         l_n2 = load_list("l_n2", n2)
         gn_sb = tile("gn_sb", [P, PACK], F32)
-        load_rows(gn_sb[:], gn)
-        w3w_raw = load_words(nc.sync, "w3w_raw", w3_words)
+        load_rows(nc.sync, gn_sb[:], gn)
         load_scales(w3s_raw, w3_scales)
-        slopes = tile("slopes", [P, 2, 8], F32)
-        load_rows(slopes[:, 0, 0:PACK], sl)
-        load_rows(slopes[:, 1, 0:PACK], sl2)
-        ths = tile("ths", [P, 2, 8], F32)
-        load_rows(ths[:, 0, 0:PACK], th)
-        load_rows(ths[:, 1, 0:PACK], th2)
+        slopes = tile("slopes", [P, 2, ROW_PITCH], F32)
+        load_rows(nc.sync, slopes[:, 0, 0:PACK], sl)
+        load_rows(nc.sync, slopes[:, 1, 0:PACK], sl2)
+        ths = tile("ths", [P, 2, ROW_PITCH], F32)
+        load_rows(nc.sync, ths[:, 0, 0:PACK], th)
+        load_rows(nc.sync, ths[:, 1, 0:PACK], th2)
         l_n6 = load_list("l_n6", n6)
         l_n5 = load_list("l_n5", n5)
 
-        def windows(name, width=2 * S):
-            return [tile("%s%d" % (name, t), [P, width], F32) for t in range(PACK)]
-
-        d_win, y_win, st_win, a_win, b_win = windows("d"), windows("y"), windows("st"), windows("a", S), windows("b")
-        st_far = tile("st_far", [P, PACK, S], F32)
-        for win in d_win + y_win:
-            nc.vector.memset(win[:, high], 0.0)
+        d_win, y_win, st_win = windows("d", 2 * S), windows("y", 2 * S), windows("st", 2 * S)
+        a_win, b_win = windows("a", S), windows("b", 2 * S)
+        for win in d_win:
+            nc.vector.memset(win[:, spare_part], 0.0)
+        half_d = [win[:, spare_part] for win in y_win]
+        y_far = [win[:, spare_part] for win in st_win]
+        st_far = [win[:, spare_part] for win in b_win]
 
         w2w = deal_words(nc.scalar.copy, "w2w", w2w_raw)
-        w2s = deal_bytes(nc.vector.tensor_copy, "w2s", w2s_raw)
-        two_w = gather("two_w", U32, xw, l_two)
-        two_s = gather("two_s", U8, xs, l_two)
+        w2s = deal_bytes("w2s", w2s_raw)
+        two_w = gather_packed("two_w", U32, xw, l_two)
+        two_s = gather_packed("two_s", U8, xs, l_two)
         neg_taus = tile("neg_taus", [P, 2, PACK], F32)
         nc.scalar.activation(neg_taus[:], taus[:, :, 0:PACK], ACT.Copy, scale=-1.0)
         w1w = deal_words(nc.scalar.copy, "w1w", w1w_raw)
-        w1s = deal_bytes(nc.vector.tensor_copy, "w1s", w1s_raw)
+        w3w = deal_words(nc.scalar.copy, "w3w", w3w_raw)
+        w1s = deal_bytes("w1s", w1s_raw)
         half_gs = tile("half_gs", [P, PACK], F32)
         nc.vector.tensor_scalar(half_gs[:], gs_sb[:], 0.5, 0.0, ALU.mult, ALU.add)
 
@@ -146,84 +163,65 @@ def tile_picked_tfcdcxbhopmneos_none_po_kernel(
         top = tile("top", [P, PACK], F32)
 
         def empty_d(t):
-            nc.vector.tensor_scalar(d_win[t][:, low], d_ps[t][:], 1.0, None, ALU.mult, ALU.max, accum_out=top[:, t : t + 1])
-            (nc.gpsimd if t in (0,1) else nc.vector).tensor_scalar(b_win[t][:, high], d_win[t][:, low], half_gs[:, t : t + 1], 0.0, ALU.mult, ALU.add)
+            nc.vector.tensor_scalar(
+                d_win[t][:, rows_part], d_ps[t][:], 1.0, None, ALU.mult, ALU.max, accum_out=top[:, t : t + 1]
+            )
+            engine = nc.gpsimd if t < HALF_D_ON_GPSIMD else nc.vector
+            engine.tensor_scalar(half_d[t], d_win[t][:, rows_part], half_gs[:, t : t + 1], 0.0, ALU.mult, ALU.add)
 
-        offs_w = gather("offs_w", U32, xw, l_offs)
+        offs_w = gather_packed("offs_w", U32, xw, l_offs)
         empty_d(0)
-        offs_s = gather("offs_s", U8, xs, l_offs, "two_s")
+        offs_s = gather_packed("offs_s", U8, xs, l_offs, tag="two_s")
         for t in range(PACK):
             product(y_ps[t][:], w1w, w1s, t, offs_w[:], offs_s[:])
         for t in range(1, PACK):
             empty_d(t)
-        cand_w = deal_words(nc.vector.tensor_copy, "cand_w", gather("cand_w_raw", U32, xw, l_cand))
-        cand_s = deal_bytes(nc.vector.tensor_copy, "cand_s", gather("cand_s_raw", U8, xs, l_cand))
-
-        Y_ON_S, N1_ON_S, N2_ON_S, A_ON_S, B_ON_S = (2,3), (), (0,1,2,3), (), (0,1,2,3)
-        sub_engine = nc.vector
-        add_engine = nc.vector
-
-        def fetch(on_scalar, dst, win, lst):
-            if on_scalar:
-                nc.scalar.activation(dst, win[:].indirect(lst[:]), ACT.Copy)
-            else:
-                nc.vector.tensor_copy(dst, win[:].indirect(lst[:]))
+        cand_w = deal_words(nc.vector.tensor_copy, "cand_w", gather_packed("cand_w_raw", U32, xw, l_cand))
+        cand_s = deal_bytes("cand_s", gather_packed("cand_s_raw", U8, xs, l_cand))
 
         exp_bias = tile("exp_bias", [P, PACK, 2], F32)
-        e = tile("e", [P, PACK, 2, S], F32)
+        soft = tile("soft", [P, PACK, 2, S], F32)
         for t in range(PACK):
             nc.scalar.activation(exp_bias[:, t, :], neg_taus[:, :, t], ACT.Copy, scale=top[:, t : t + 1])
-            for k, lst in enumerate((l_n3, l_n4)):
+            for k, offsets in enumerate((l_n3, l_n4)):
                 nc.scalar.activation(
-                    e[:, t, k, :], d_win[t][:].indirect(lst[:]), ACT.Exp,
+                    soft[:, t, k, :], d_win[t][:].indirect(offsets[:]), ACT.Exp,
                     bias=exp_bias[:, t, k : k + 1], scale=taus[:, k, t : t + 1],
                 )
-            if t in Y_ON_S:
-                nc.scalar.copy(y_win[t][:, low], y_ps[t][:])
-            else:
-                nc.vector.tensor_copy(y_win[t][:, low], y_ps[t][:])
-            if t in N1_ON_S:
-                fetch(True, st_win[t][:, high], y_win[t], l_n1)
-        w3s = deal_bytes(nc.vector.tensor_copy, "w3s", w3s_raw)
-
+            nc.vector.tensor_copy(y_win[t][:, rows_part], y_ps[t][:])
+        w3s = deal_bytes("w3s", w3s_raw)
         for t in range(PACK):
-            if t not in N1_ON_S:
-                fetch(False, st_win[t][:, high], y_win[t], l_n1)
-            nc.vector.tensor_tensor(st_win[t][:, low], st_win[t][:, high], y_ps[t][:], ALU.max)
+            nc.vector.tensor_copy(y_far[t], y_win[t][:].indirect(l_n1[:]))
+            nc.vector.tensor_tensor(st_win[t][:, rows_part], y_far[t], y_ps[t][:], ALU.max)
         sig_bias = tile("sig_bias", [P, 2, PACK], F32)
         nc.vector.scalar_tensor_tensor(sig_bias[:], slopes[:, :, 0:PACK], -1.0, ths[:, :, 0:PACK], ALU.mult, ALU.mult)
 
-        diff = tile("diff", [P, PACK, S], F32)
+        pair = tile("pair", [P, PACK, S], F32)
         z2_rows = tile("z2_rows", [P, PACK, S], BF16)
-        def half_banks(name, tag):
-            banks = [psum.tile([P, 2, HALF], F32, name="%s%d" % (name, k), tag="%s%d" % (tag, k)) for k in range(PACK)]
-            return banks, [[banks[2 * h + t // 2][:, t % 2, :] for t in range(PACK)] for h in range(2)]
-
         b_banks, b_ps = half_banks("b_ps", "left")
-        for h in range(2):
-            nc.scalar.activation(e[:, :, :, halves[h]], e[:, :, :, halves[h]], ACT.Ln, bias=0.25)
-        for h in range(2):
+        for cols in halves:
+            nc.scalar.activation(soft[:, :, :, cols], soft[:, :, :, cols], ACT.Ln, bias=0.25)
+        for h, weave in enumerate((nc.vector.tensor_copy, nc.scalar.copy)):
             cols = halves[h]
-            for u in range(0, PACK, 4):
-                (nc.gpsimd if h in () else nc.vector).tensor_tensor(diff[:, u : u + 4, cols], e[:, u : u + 4, 0, cols], e[:, u : u + 4, 1, cols], ALU.subtract)
+            nc.vector.tensor_tensor(pair[:, :, cols], soft[:, :, 0, cols], soft[:, :, 1, cols], ALU.subtract)
             for t in range(PACK):
                 nc.vector.scalar_tensor_tensor(
-                    z2_rows[:, t, cols], diff[:, t, cols], gs_sb[:, t : t + 1], b_win[t][:, high][:, cols], ALU.mult, ALU.add
+                    z2_rows[:, t, cols], pair[:, t, cols], gs_sb[:, t : t + 1], half_d[t][:, cols], ALU.mult, ALU.add
                 )
             z2_in = tile("z2_in%d" % h, [P, HALF * PACK], BF16)
             z2_w = tile("z2_w%d" % h, [P, HALF], U32)
             z2_s = tile("z2_s%d" % h, [P, HALF], U8)
-            (nc.scalar.copy if h in (1,) else nc.vector.tensor_copy)(woven(z2_in[:]), planar(z2_rows, cols))
+            weave(woven(z2_in[:]), row_tiles(z2_rows, cols))
             nc.vector.quantize_mx(z2_w[:].bitcast(FP8X4), z2_s[:], z2_in[:])
             for t in range(PACK):
                 product(b_ps[h][t], cand_w, cand_s, t, z2_w[:], z2_s[:])
         for t in range(PACK):
-            fetch(t in N2_ON_S, st_far[:, t, :], st_win[t], l_n2)
-        w3w = deal_words(nc.scalar.copy, "w3w", w3w_raw)
+            nc.scalar.activation(st_far[t], st_win[t][:].indirect(l_n2[:]), ACT.Copy)
+
         sg2 = tile("sg2", [P, PACK, S], F32)
         for h in range(2):
             for t in range(PACK):
-                if 4 * h + t in B_ON_S:
+                if h == 0 or t == PACK - 1:
                     nc.scalar.activation(b_win[t][:, halves[h]], b_ps[h][t], ACT.Copy, scale=0.0625)
                 else:
                     nc.vector.tensor_scalar(b_win[t][:, halves[h]], b_ps[h][t], 0.0625, None, ALU.mult)
@@ -233,61 +231,58 @@ def tile_picked_tfcdcxbhopmneos_none_po_kernel(
                 bias=sig_bias[:, 1, t : t + 1], scale=slopes[:, 1, t : t + 1],
             )
 
-        least = diff
         for t in range(PACK):
-            nc.vector.tensor_tensor(least[:, t, :], st_win[t][:, low], st_far[:, t, :], ALU.min)
+            nc.vector.tensor_tensor(pair[:, t, :], st_win[t][:, rows_part], st_far[t], ALU.min)
         a_banks, a_ps = half_banks("a_ps", "right")
-        gn_view = gn_sb[:].unsqueeze(1).unsqueeze(3).to_broadcast([P, HALF // 4, PACK, 4])
+        gn_view = gn_sb[:].unsqueeze(1).unsqueeze(3).to_broadcast([P, HALF // LINE, PACK, LINE])
         for h in range(2):
-            z_in = tile("z_in%d" % h, [P, HALF * PACK], BF16, "z_in")
+            z_in = tile("z_in%d" % h, [P, HALF * PACK], BF16, tag="z_in")
             z_w = tile("z_w%d" % h, [P, HALF], U32)
             z_s = tile("z_s%d" % h, [P, HALF], U8)
-            nc.vector.tensor_tensor(woven(z_in[:]), planar(least, halves[h]), gn_view, ALU.mult)
+            nc.vector.tensor_tensor(woven(z_in[:]), row_tiles(pair, halves[h]), gn_view, ALU.mult)
             nc.vector.quantize_mx(z_w[:].bitcast(FP8X4), z_s[:], z_in[:])
             for t in range(PACK):
                 product(a_ps[h][t], w3w, w3s, t, z_w[:], z_s[:])
 
         sg = tile("sg", [P, PACK, S], F32)
-        p1 = tile("p1", [P, PACK, S], F32)
-        p2 = tile("p2", [P, PACK, S], F32)
+        sg_b = tile("sg_b", [P, PACK, S], F32)
+        sg2_a = tile("sg2_a", [P, PACK, S], F32)
         res = tile("res", [P, PACK, S], F32)
         for h in range(2):
             for t in range(PACK):
-                if 4 * h + t in A_ON_S:
-                    nc.scalar.copy(a_win[t][:, halves[h]], a_ps[h][t])
-                else:
-                    nc.vector.tensor_copy(a_win[t][:, halves[h]], a_ps[h][t])
-        for h in range(2):
-            for u in range(2):
-                if 2 * h + u in (0,1):
-                    for t in (2 * u, 2 * u + 1):
-                        nc.gpsimd.tensor_tensor(p2[:, t, halves[h]], sg2[:, t, halves[h]], a_win[t][:, halves[h]], ALU.mult)
-                    continue
-                nc.vector.tensor_tensor(p2[:, 2 * u : 2 * u + 2, halves[h]], sg2[:, 2 * u : 2 * u + 2, halves[h]], a_banks[2 * h + u][:], ALU.mult)
+                nc.vector.tensor_copy(a_win[t][:, halves[h]], a_ps[h][t])
+        first, second = halves
+        for t in range(PACK):
+            nc.gpsimd.tensor_tensor(sg2_a[:, t, first], sg2[:, t, first], a_win[t][:, first], ALU.mult)
+        for u in range(2):
+            rows = slice(2 * u, 2 * u + 2)
+            nc.vector.tensor_tensor(sg2_a[:, rows, second], sg2[:, rows, second], a_banks[2 + u][:], ALU.mult)
+
         out_rows = out_0.rearrange("(p t) j -> p t j", t=PACK)
         out_words = out_1[0].rearrange("p n r -> p (n r)").bitcast(I32)
         res_w = tile("res_w", [P, S], U32)
         res_s = tile("res_s", [P, S], U8)
-        for c, (first, last, group, adder, weaver) in enumerate([(0, 256, 2, nc.vector, nc.scalar.copy), (256, 512, 2, nc.vector, nc.vector.tensor_copy)]):
-            cols, h = slice(first, last), first // HALF
-            part = slice(first - h * HALF, last - h * HALF)
+        plans = ((2, nc.gpsimd, nc.scalar.copy), (1, nc.vector, nc.vector.tensor_copy))
+        for h, (group, adder, weave) in enumerate(plans):
+            cols = halves[h]
             for t in range(PACK):
                 nc.scalar.activation(
-                    sg[:, t, cols], a_win[t][:].indirect(l_n5[:, first // 16 : last // 16]), ACT.Sigmoid,
+                    sg[:, t, cols], a_win[t][:].indirect(l_n5[:, cols.start // 16 : cols.stop // 16]), ACT.Sigmoid,
                     bias=sig_bias[:, 0, t : t + 1], scale=slopes[:, 0, t : t + 1],
                 )
-                if (t + 1) % group:
-                    continue
-                rows = slice(t + 1 - group, t + 1)
-                b_part = b_banks[2 * h + t // 2][:, slice(t % 2 + 1 - group, t % 2 + 1), part]
-                nc.vector.scalar_tensor_tensor(p1[:, rows, cols], b_part, 0.0625, sg[:, rows, cols], ALU.mult, ALU.mult)
-                adder.tensor_tensor(res[:, rows, cols], p1[:, rows, cols], p2[:, rows, cols], ALU.add)
-                if t % 2:
+                if (t + 1) % group == 0:
+                    rows = slice(t + 1 - group, t + 1)
+                    b_part = b_banks[2 * h + t // 2][:, t % 2 + 1 - group : t % 2 + 1, :]
+                    nc.vector.scalar_tensor_tensor(
+                        sg_b[:, rows, cols], b_part, 0.0625, sg[:, rows, cols], ALU.mult, ALU.mult
+                    )
+                    adder.tensor_tensor(res[:, rows, cols], sg_b[:, rows, cols], sg2_a[:, rows, cols], ALU.add)
+                if t % 2 == 1:
                     nc.sync.dma_start(out_rows[:, t - 1 : t + 1, cols], res[:, t - 1 : t + 1, cols])
-            res_in = tile("res_in%d" % c, [P, (last - first) * PACK], BF16)
-            weaver(woven(res_in[:]), planar(res, cols))
+            res_in = tile("res_in%d" % h, [P, HALF * PACK], BF16)
+            weave(woven(res_in[:]), row_tiles(res, cols))
             nc.vector.quantize_mx(res_w[:, cols].bitcast(FP8X4), res_s[:, cols], res_in[:])
             nc.sync.dma_start(out_words[:, cols], res_w[:, cols].bitcast(I32))
-        for q in range(4):
+        for q in range(QUADRANTS):
             queue = nc.scalar if q % 2 == 0 else nc.sync
             queue.dma_start(out_2[0, 4 * q : 4 * q + 4, :].bitcast(I32), res_s[32 * q : 32 * q + 4, :].bitcast(I32))

from contextlib import ExitStack

import concourse.mybir as mybir

F32 = mybir.dt.float32
BF16 = mybir.dt.bfloat16
I32 = mybir.dt.int32
U32 = mybir.dt.uint32
U16 = mybir.dt.uint16
U8 = mybir.dt.uint8
FP8X4 = mybir.dt.float8_e4m3fn_x4
ALU = mybir.AluOpType
ACT = mybir.ActivationFunctionType

P = 128
PACK = 4
QUADRANTS = 4
T = 2048
S = 512
HALF = S // 2
LINE = 4
ROW_PITCH = 8
HALF_D_ON_GPSIMD = 2
FLOPS = 4 * 2 * S * S * S


def tile_picked_tfcdcxbhopmneos_none_po_kernel(
    tc, x_words, x_scales, w1_words, w1_scales, w2_words, w2_scales, tau, tau2, gn, w3_words, w3_scales,
    gs, sl, th, sl2, th2, offs, two, n1, n2, n3, n4, cand, n5, n6, out_0, out_1, out_2,
):
    nc = tc.nc
    with ExitStack() as ctx:
        keep = ctx.enter_context(tc.tile_pool(name="keep", bufs=1))
        psum = ctx.enter_context(tc.psum_pool(name="psum", bufs=1))

        def tile(name, shape, dtype, tag=None):
            return keep.tile(shape, dtype, name=name, tag=tag or name, align_bytes=64)

        def load_list(name, src):
            dst = tile(name, [P, S // 16], U16)
            nc.sync.dma_start(dst[:], src)
            return dst

        def load_words(queue, name, src):
            dst = tile(name, [P, src.shape[2]], U32)
            queue.dma_start(dst[:].bitcast(I32), src[0].rearrange("p n r -> p (n r)").bitcast(I32))
            return dst

        def zeroed_scale_tile(engine, name, width):
            dst = tile(name, [P, width], U8)
            engine.memset(dst[:].bitcast(I32), 0)
            return dst

        def load_scales(dst, src):
            for q in range(QUADRANTS):
                nc.sync.dma_start(dst[32 * q : 32 * q + 4, :].bitcast(I32), src[0, 4 * q : 4 * q + 4, :].bitcast(I32))

        def load_rows(queue, dst, src):
            queue.dma_start(dst, src.rearrange("(p t) o -> p (t o)", t=PACK))

        def deal_words(copy, name, src):
            dst = tile(name, [P, S], U32)
            copy(
                dst[:].rearrange("p (t c i) -> p c t i", t=PACK, i=LINE),
                src[:].rearrange("p (c i t) -> p c t i", t=PACK, i=LINE),
            )
            return dst

        def deal_bytes(name, src):
            dst = tile(name, [P, S], U8)
            nc.vector.tensor_copy(
                dst[:].rearrange("p (t m) -> p t m", t=PACK), src[:].rearrange("p (m t) -> p t m", t=PACK)
            )
            return dst

        def gather_packed(name, dtype, window, offsets, tag=None):
            dst = tile(name, [P, S], dtype, tag)
            nc.vector.tensor_copy(dst[:], window[:].indirect(offsets[:]))
            return dst

        def product(out, lhs_words, lhs_bytes, t, rhs_words, rhs_bytes):
            cols = slice(t * P, (t + 1) * P)
            nc.tensor.matmul_mx(
                out=out, lhsT=lhs_words[:, cols].bitcast(FP8X4), lhsT_scale=lhs_bytes[:, cols],
                rhs=rhs_words.bitcast(FP8X4), rhs_scale=rhs_bytes, start=True, stop=True,
            )

        def row_tiles(src, cols):
            return src[:, :, cols].rearrange("p t (c i) -> p c t i", i=LINE)

        def woven(dst):
            return dst.rearrange("p (c i t) -> p c t i", t=PACK, i=LINE)

        def windows(name, width):
            return [tile("%s%d" % (name, t), [P, width], F32) for t in range(PACK)]

        def half_banks(name, tag):
            banks = [psum.tile([P, 2, HALF], F32, name="%s%d" % (name, k), tag="%s%d" % (tag, k)) for k in range(PACK)]
            return banks, [[banks[2 * h + t // 2][:, t % 2, :] for t in range(PACK)] for h in range(2)]

        halves = [slice(0, HALF), slice(HALF, S)]
        rows_part, spare_part = slice(0, S), slice(S, 2 * S)

        w2s_raw = zeroed_scale_tile(nc.gpsimd, "w2s_raw", S)
        xs = zeroed_scale_tile(nc.gpsimd, "xs", T)
        w1s_raw = zeroed_scale_tile(nc.vector, "w1s_raw", S)
        w3s_raw = zeroed_scale_tile(nc.vector, "w3s_raw", S)
        taus = tile("taus", [P, 2, ROW_PITCH], F32)
        load_rows(nc.scalar, taus[:, 0, 0:PACK], tau)
        load_rows(nc.scalar, taus[:, 1, 0:PACK], tau2)
        xw = load_words(nc.scalar, "xw", x_words)
        l_two = load_list("l_two", two)
        load_scales(w2s_raw, w2_scales)
        load_scales(xs, x_scales)
        l_n3 = load_list("l_n3", n3)
        w2w_raw = load_words(nc.sync, "w2w_raw", w2_words)
        l_offs = load_list("l_offs", offs)
        l_n4 = load_list("l_n4", n4)
        gs_sb = tile("gs_sb", [P, PACK], F32)
        load_rows(nc.sync, gs_sb[:], gs)
        w1w_raw = load_words(nc.sync, "w1w_raw", w1_words)
        w3w_raw = load_words(nc.sync, "w3w_raw", w3_words)
        load_scales(w1s_raw, w1_scales)
        l_cand = load_list("l_cand", cand)
        l_n1 = load_list("l_n1", n1)
        l_n2 = load_list("l_n2", n2)
        gn_sb = tile("gn_sb", [P, PACK], F32)
        load_rows(nc.sync, gn_sb[:], gn)
        load_scales(w3s_raw, w3_scales)
        slopes = tile("slopes", [P, 2, ROW_PITCH], F32)
        load_rows(nc.sync, slopes[:, 0, 0:PACK], sl)
        load_rows(nc.sync, slopes[:, 1, 0:PACK], sl2)
        ths = tile("ths", [P, 2, ROW_PITCH], F32)
        load_rows(nc.sync, ths[:, 0, 0:PACK], th)
        load_rows(nc.sync, ths[:, 1, 0:PACK], th2)
        l_n6 = load_list("l_n6", n6)
        l_n5 = load_list("l_n5", n5)

        d_win, y_win, st_win = windows("d", 2 * S), windows("y", 2 * S), windows("st", 2 * S)
        a_win, b_win = windows("a", S), windows("b", 2 * S)
        for win in d_win:
            nc.vector.memset(win[:, spare_part], 0.0)
        half_d = [win[:, spare_part] for win in y_win]
        y_far = [win[:, spare_part] for win in st_win]
        st_far = [win[:, spare_part] for win in b_win]

        w2w = deal_words(nc.scalar.copy, "w2w", w2w_raw)
        w2s = deal_bytes("w2s", w2s_raw)
        two_w = gather_packed("two_w", U32, xw, l_two)
        two_s = gather_packed("two_s", U8, xs, l_two)
        neg_taus = tile("neg_taus", [P, 2, PACK], F32)
        nc.scalar.activation(neg_taus[:], taus[:, :, 0:PACK], ACT.Copy, scale=-1.0)
        w1w = deal_words(nc.scalar.copy, "w1w", w1w_raw)
        w3w = deal_words(nc.scalar.copy, "w3w", w3w_raw)
        w1s = deal_bytes("w1s", w1s_raw)
        half_gs = tile("half_gs", [P, PACK], F32)
        nc.vector.tensor_scalar(half_gs[:], gs_sb[:], 0.5, 0.0, ALU.mult, ALU.add)

        d_ps = [psum.tile([P, S], F32, name="d_ps%d" % t, tag="left%d" % t) for t in range(PACK)]
        y_ps = [psum.tile([P, S], F32, name="y_ps%d" % t, tag="right%d" % t) for t in range(PACK)]
        for t in range(PACK):
            product(d_ps[t][:], w2w, w2s, t, two_w[:], two_s[:])
        top = tile("top", [P, PACK], F32)

        def empty_d(t):
            nc.vector.tensor_scalar(
                d_win[t][:, rows_part], d_ps[t][:], 1.0, None, ALU.mult, ALU.max, accum_out=top[:, t : t + 1]
            )
            engine = nc.gpsimd if t < HALF_D_ON_GPSIMD else nc.vector
            engine.tensor_scalar(half_d[t], d_win[t][:, rows_part], half_gs[:, t : t + 1], 0.0, ALU.mult, ALU.add)

        offs_w = gather_packed("offs_w", U32, xw, l_offs)
        empty_d(0)
        offs_s = gather_packed("offs_s", U8, xs, l_offs, tag="two_s")
        for t in range(PACK):
            product(y_ps[t][:], w1w, w1s, t, offs_w[:], offs_s[:])
        for t in range(1, PACK):
            empty_d(t)
        cand_w = deal_words(nc.vector.tensor_copy, "cand_w", gather_packed("cand_w_raw", U32, xw, l_cand))
        cand_s = deal_bytes("cand_s", gather_packed("cand_s_raw", U8, xs, l_cand))

        exp_bias = tile("exp_bias", [P, PACK, 2], F32)
        soft = tile("soft", [P, PACK, 2, S], F32)
        for t in range(PACK):
            nc.scalar.activation(exp_bias[:, t, :], neg_taus[:, :, t], ACT.Copy, scale=top[:, t : t + 1])
            for k, offsets in enumerate((l_n3, l_n4)):
                nc.scalar.activation(
                    soft[:, t, k, :], d_win[t][:].indirect(offsets[:]), ACT.Exp,
                    bias=exp_bias[:, t, k : k + 1], scale=taus[:, k, t : t + 1],
                )
            nc.vector.tensor_copy(y_win[t][:, rows_part], y_ps[t][:])
        w3s = deal_bytes("w3s", w3s_raw)
        for t in range(PACK):
            nc.vector.tensor_copy(y_far[t], y_win[t][:].indirect(l_n1[:]))
            nc.vector.tensor_tensor(st_win[t][:, rows_part], y_far[t], y_ps[t][:], ALU.max)
        sig_bias = tile("sig_bias", [P, 2, PACK], F32)
        nc.vector.scalar_tensor_tensor(sig_bias[:], slopes[:, :, 0:PACK], -1.0, ths[:, :, 0:PACK], ALU.mult, ALU.mult)

        pair = tile("pair", [P, PACK, S], F32)
        z2_rows = tile("z2_rows", [P, PACK, S], BF16)
        b_banks, b_ps = half_banks("b_ps", "left")
        for cols in halves:
            nc.scalar.activation(soft[:, :, :, cols], soft[:, :, :, cols], ACT.Ln, bias=0.25)
        for h, weave in enumerate((nc.vector.tensor_copy, nc.scalar.copy)):
            cols = halves[h]
            nc.vector.tensor_tensor(pair[:, :, cols], soft[:, :, 0, cols], soft[:, :, 1, cols], ALU.subtract)
            for t in range(PACK):
                nc.vector.scalar_tensor_tensor(
                    z2_rows[:, t, cols], pair[:, t, cols], gs_sb[:, t : t + 1], half_d[t][:, cols], ALU.mult, ALU.add
                )
            z2_in = tile("z2_in%d" % h, [P, HALF * PACK], BF16)
            z2_w = tile("z2_w%d" % h, [P, HALF], U32)
            z2_s = tile("z2_s%d" % h, [P, HALF], U8)
            weave(woven(z2_in[:]), row_tiles(z2_rows, cols))
            nc.vector.quantize_mx(z2_w[:].bitcast(FP8X4), z2_s[:], z2_in[:])
            for t in range(PACK):
                product(b_ps[h][t], cand_w, cand_s, t, z2_w[:], z2_s[:])
        for t in range(PACK):
            nc.scalar.activation(st_far[t], st_win[t][:].indirect(l_n2[:]), ACT.Copy)

        sg2 = tile("sg2", [P, PACK, S], F32)
        for h in range(2):
            for t in range(PACK):
                if h == 0 or t == PACK - 1:
                    nc.scalar.activation(b_win[t][:, halves[h]], b_ps[h][t], ACT.Copy, scale=0.0625)
                else:
                    nc.vector.tensor_scalar(b_win[t][:, halves[h]], b_ps[h][t], 0.0625, None, ALU.mult)
        for t in range(PACK):
            nc.scalar.activation(
                sg2[:, t, :], b_win[t][:].indirect(l_n6[:]), ACT.Sigmoid,
                bias=sig_bias[:, 1, t : t + 1], scale=slopes[:, 1, t : t + 1],
            )

        for t in range(PACK):
            nc.vector.tensor_tensor(pair[:, t, :], st_win[t][:, rows_part], st_far[t], ALU.min)
        a_banks, a_ps = half_banks("a_ps", "right")
        gn_view = gn_sb[:].unsqueeze(1).unsqueeze(3).to_broadcast([P, HALF // LINE, PACK, LINE])
        for h in range(2):
            z_in = tile("z_in%d" % h, [P, HALF * PACK], BF16, tag="z_in")
            z_w = tile("z_w%d" % h, [P, HALF], U32)
            z_s = tile("z_s%d" % h, [P, HALF], U8)
            nc.vector.tensor_tensor(woven(z_in[:]), row_tiles(pair, halves[h]), gn_view, ALU.mult)
            nc.vector.quantize_mx(z_w[:].bitcast(FP8X4), z_s[:], z_in[:])
            for t in range(PACK):
                product(a_ps[h][t], w3w, w3s, t, z_w[:], z_s[:])

        sg = tile("sg", [P, PACK, S], F32)
        sg_b = tile("sg_b", [P, PACK, S], F32)
        sg2_a = tile("sg2_a", [P, PACK, S], F32)
        res = tile("res", [P, PACK, S], F32)
        for h in range(2):
            for t in range(PACK):
                nc.vector.tensor_copy(a_win[t][:, halves[h]], a_ps[h][t])
        first, second = halves
        for t in range(PACK):
            nc.gpsimd.tensor_tensor(sg2_a[:, t, first], sg2[:, t, first], a_win[t][:, first], ALU.mult)
        for u in range(2):
            rows = slice(2 * u, 2 * u + 2)
            nc.vector.tensor_tensor(sg2_a[:, rows, second], sg2[:, rows, second], a_banks[2 + u][:], ALU.mult)

        out_rows = out_0.rearrange("(p t) j -> p t j", t=PACK)
        out_words = out_1[0].rearrange("p n r -> p (n r)").bitcast(I32)
        res_w = tile("res_w", [P, S], U32)
        res_s = tile("res_s", [P, S], U8)
        plans = ((2, nc.gpsimd, nc.scalar.copy), (1, nc.vector, nc.vector.tensor_copy))
        for h, (group, adder, weave) in enumerate(plans):
            cols = halves[h]
            for t in range(PACK):
                nc.scalar.activation(
                    sg[:, t, cols], a_win[t][:].indirect(l_n5[:, cols.start // 16 : cols.stop // 16]), ACT.Sigmoid,
                    bias=sig_bias[:, 0, t : t + 1], scale=slopes[:, 0, t : t + 1],
                )
                if (t + 1) % group == 0:
                    rows = slice(t + 1 - group, t + 1)
                    b_part = b_banks[2 * h + t // 2][:, t % 2 + 1 - group : t % 2 + 1, :]
                    nc.vector.scalar_tensor_tensor(
                        sg_b[:, rows, cols], b_part, 0.0625, sg[:, rows, cols], ALU.mult, ALU.mult
                    )
                    adder.tensor_tensor(res[:, rows, cols], sg_b[:, rows, cols], sg2_a[:, rows, cols], ALU.add)
                if t % 2 == 1:
                    nc.sync.dma_start(out_rows[:, t - 1 : t + 1, cols], res[:, t - 1 : t + 1, cols])
            res_in = tile("res_in%d" % h, [P, HALF * PACK], BF16)
            weave(woven(res_in[:]), row_tiles(res, cols))
            nc.vector.quantize_mx(res_w[:, cols].bitcast(FP8X4), res_s[:, cols], res_in[:])
            nc.sync.dma_start(out_words[:, cols], res_w[:, cols].bitcast(I32))
        for q in range(QUADRANTS):
            queue = nc.scalar if q % 2 == 0 else nc.sync
            queue.dma_start(out_2[0, 4 * q : 4 * q + 4, :].bitcast(I32), res_s[32 * q : 32 * q + 4, :].bitcast(I32))
